import numpy as np
import ml_dtypes


def mxq(x, axis, fmt="e4m3"):
    dtype, down = {"e4m3": (ml_dtypes.float8_e4m3fn, 7), "e5m2": (ml_dtypes.float8_e5m2, 14)}[fmt]
    v = np.moveaxis(np.asarray(x, np.float32).astype(ml_dtypes.bfloat16).astype(np.float64), axis, -1)
    blocks = v.reshape(v.shape[:-1] + (-1, 32))
    amax = np.abs(blocks).max(-1, keepdims=True)
    byte = np.maximum(np.where(amax > 0, np.frexp(amax)[1] - 1 + 127, 0) - down, 1)
    scale = np.exp2(byte - 127.0)
    codes = (blocks / scale).astype(np.float32).astype(dtype).astype(np.float64)
    return np.moveaxis((codes * scale).reshape(v.shape), -1, axis)


WIDE = False


def mx_kscale(k):
    if not WIDE:
        return np.ones(k)
    levels = np.array([30, -30])
    if k % 512:
        return np.exp2(np.random.permutation(np.resize(levels, k // 32))).repeat(32)
    a = np.empty((k // 512, 16))
    for p in range(k // 512):
        a[p, :8] = np.random.permutation(np.resize(levels, 8))
        for g in range(8):
            far = levels[np.abs(levels - a[p, g]) >= 10]
            a[p, g + 8] = far[np.random.randint(len(far))]
    return np.exp2(a.ravel()).repeat(32)


def f64(x):
    return np.asarray(x).astype(np.float64)


E2M1 = np.array([0.0, 0.5, 1.0, 1.5, 2.0, 3.0, 4.0, 6.0, -0.0, -0.5, -1.0, -1.5, -2.0, -3.0, -4.0, -6.0])


def pack_weight(w, fmt):
    k, n = w.shape
    w = f64(np.asarray(w, np.float32).astype(ml_dtypes.bfloat16)).reshape(k // 32, 32, n)
    amax = np.abs(w).max(1)
    if fmt == "e4m3":
        byte = np.frexp(amax)[1] - 1 + 127 - 7
    else:
        mant, ex = np.frexp(amax / 6.0)
        byte = np.where(mant > 0.5, ex, ex - 1) + 127
    byte = np.clip(np.where(amax > 0, byte, 1), 1, 254)
    scaled = (w * np.exp2(127.0 - byte)[:, None, :]).reshape(k, n).astype(np.float32)
    by_word = np.ascontiguousarray(scaled.reshape(k // 512, 128, 4, n).transpose(0, 1, 3, 2))
    if fmt == "e4m3":
        words = by_word.astype(ml_dtypes.float8_e4m3fn).view(np.uint8)
    else:
        c = by_word.astype(ml_dtypes.float4_e2m1fn).view(np.uint8) & 0xF
        words = (c[..., 0::2] | (c[..., 1::2] << 4)).reshape(k // 512, 128, 2 * n)
    return np.ascontiguousarray(words), np.ascontiguousarray(byte.astype(np.uint8).reshape(k // 512, 16, n))


def unpack_weight(words, scales, fmt):
    g, _, n = scales.shape
    words = np.ascontiguousarray(words).reshape(g, 128, n, -1)
    if fmt == "e4m3":
        vals = words.view(ml_dtypes.float8_e4m3fn).astype(np.float64)
    else:
        nib = np.empty((g, 128, n, 4), np.uint8)
        nib[..., 0::2] = words & 0xF
        nib[..., 1::2] = words >> 4
        vals = E2M1[nib]
    vals = vals * np.repeat(np.exp2(scales.astype(np.float64) - 127.0), 8, axis=1)[..., None]
    return vals.transpose(0, 1, 3, 2).reshape(g * 512, n)


O, T, D, H = 1024, 1536, 256, 1536


def setup_inputs():
    n = np.random.standard_normal
    s = mx_kscale(T)[:, None]
    m = np.exp(0.5 * n((T, 1)))
    x = n((T, D)) * s
    p_x4 = pack_weight(x[:O], "e2m1")
    return {
        "x4_words": p_x4[0],
        "x4_scales": p_x4[1],
        "x8": (x[O:]).astype(np.float32),
        "dy": (m * n((T, H)) / np.sqrt(T) / s).astype(np.float32),
        "w": (0.1 * n((256, 1536))).astype(np.float32),
    }


def reference(x4_words, x4_scales, x8, dy, w):
    x4_ = unpack_weight(x4_words, x4_scales, "e2m1")
    x8_ = mxq(f64(x8), 0, "e4m3")
    dy_ = mxq(f64(dy), 0, "e5m2")
    y = x4_.T @ dy_[:O] + x8_.T @ dy_[O:]
    return f64(w) - 0.0625 * y

@@ -1,0 +1,149 @@
+from contextlib import ExitStack
+
+import concourse.mybir as mybir
+
+FLOPS = 2 * 1536 * 256 * 1536
+
+F32 = mybir.dt.float32
+BF16 = mybir.dt.bfloat16
+I32 = mybir.dt.int32
+U32 = mybir.dt.uint32
+U8 = mybir.dt.uint8
+E4M3 = mybir.dt.float8_e4m3fn_x4
+E5M2 = mybir.dt.float8_e5m2_x4
+E2M1 = mybir.dt.float4_e2m1fn_x4
+MULT = mybir.AluOpType.mult
+ADD = mybir.AluOpType.add
+
+P = 128
+N = 512
+T, D, H = 1536, 256, 1536
+
+
+def tile_mix_dwsav_sgd_kernel(tc, x4_words, x4_scales, x8, dy, w, out):
+    nc = tc.nc
+    with ExitStack() as ctx:
+        pool = ctx.enter_context(tc.tile_pool(name="pool", bufs=1))
+        psum = ctx.enter_context(tc.psum_pool(name="psum", bufs=1))
+        ctx.enter_context(tc.manual_schedule())
+
+        acc = {}
+        for c in range(3):
+            for m in range(2):
+                acc[c, m] = psum.tile([P, N], F32, name="acc_%d_%d" % (c, m))
+
+        def load_dy(g, lo, hi):
+            raw = pool.tile([P, 4, hi - lo], F32, name="raw_%d_%d" % (g, lo), align_bytes=64)
+            rows = dy[512 * g : 512 * (g + 1), lo:hi]
+            nc.sync.dma_start(out=raw[:], in_=rows.rearrange("(p j) h -> p j h", j=4))
+            return raw
+
+        x4_sc = pool.tile([P, 2, D], U8, name="x4_sc", align_bytes=64)
+        nc.vector.memset(x4_sc[:].rearrange("p a n -> p (a n)").bitcast(I32), 0)
+
+        x8_raw = pool.tile([P, 4, D], F32, name="x8_raw", align_bytes=64)
+        nc.sync.dma_start(out=x8_raw[:], in_=x8.rearrange("(p j) d -> p j d", j=4))
+        x4_wd = pool.tile([P, 2, 2 * D], U8, name="x4_wd", align_bytes=64)
+        nc.sync.dma_start(out=x4_wd[:].bitcast(I32), in_=x4_words.rearrange("a p b -> p a b").bitcast(I32))
+        raw2 = load_dy(2, 0, H)
+        for q in range(4):
+            nc.scalar.dma_start(
+                out=x4_sc[32 * q : 32 * q + 4, :, :].bitcast(I32),
+                in_=x4_scales[:, 4 * q : 4 * q + 4, :].rearrange("a r n -> r a n").bitcast(I32),
+            )
+        raw0 = load_dy(0, 0, H)
+        raw1a = load_dy(1, 0, 2 * N)
+        raw1b = load_dy(1, 2 * N, H)
+        w_sb = {}
+        for c in range(3):
+            for m in range(2):
+                w_sb[c, m] = pool.tile([P, N], F32, name="w_%d_%d" % (c, m), align_bytes=64)
+                nc.sync.dma_start(out=w_sb[c, m][:], in_=w[P * m : P * (m + 1), N * c : N * (c + 1)])
+
+        grouped, codes, scales = {}, {}, {}
+
+        def interleave(g, c, raw, col, v):
+            t = pool.tile([P, N, 4], BF16, name="grp_%d_%d" % (g, c), align_bytes=64)
+            grouped[g, c] = t
+            if v < N:
+                nc.scalar.copy(
+                    out=t[:, v:N, :].rearrange("p (c i) j -> p c j i", i=4),
+                    in_=raw[:, :, col + v : col + N].rearrange("p j (c i) -> p c j i", i=4),
+                )
+            if v > 0:
+                nc.vector.tensor_copy(
+                    out=t[:, 0:v, :].rearrange("p (c i) j -> p c j i", i=4),
+                    in_=raw[:, :, col : col + v].rearrange("p j (c i) -> p c j i", i=4),
+                )
+
+        def quantize(g, c):
+            k = pool.tile([P, N], U32, name="cod_%d_%d" % (g, c), align_bytes=64)
+            s = pool.tile([P, N], U8, name="sca_%d_%d" % (g, c), align_bytes=64)
+            nc.vector.quantize_mx(
+                out=k[:].bitcast(E5M2), scales=s[:], in_=grouped[g, c][:].rearrange("p h j -> p (h j)")
+            )
+            codes[g, c], scales[g, c] = k, s
+
+        def multiply(g, c, start, stop):
+            for m in range(2):
+                if g == 2:
+                    lhsT = x8_codes[:, P * m : P * (m + 1)].bitcast(E4M3)
+                    lhsT_scale = x8_scales[:, P * m : P * (m + 1)]
+                else:
+                    lhsT = x4_wd[:, g, 2 * P * m : 2 * P * (m + 1)].bitcast(E2M1)
+                    lhsT_scale = x4_sc[:, g, P * m : P * (m + 1)]
+                nc.tensor.matmul_mx(
+                    out=acc[c, m][:],
+                    lhsT=lhsT,
+                    lhsT_scale=lhsT_scale,
+                    rhs=codes[g, c][:].bitcast(E5M2),
+                    rhs_scale=scales[g, c][:],
+                    start=start,
+                    stop=stop,
+                )
+
+        def finish(c, m, parts=1):
+            width = N // parts
+            for i in range(parts):
+                cols = slice(width * i, width * (i + 1))
+                o = pool.tile([P, width], F32, name="o_%d_%d_%d" % (c, m, i), align_bytes=64)
+                nc.vector.scalar_tensor_tensor(
+                    out=o[:], in0=acc[c, m][:, cols], scalar=-0.0625, in1=w_sb[c, m][:, cols], op0=MULT, op1=ADD
+                )
+                h0 = N * c + width * i
+                nc.sync.dma_start(out=out[P * m : P * (m + 1), h0 : h0 + width], in_=o[:])
+
+        x8_grp = pool.tile([P, D, 4], BF16, name="x8_grp", align_bytes=64)
+        nc.scalar.copy(out=x8_grp[:], in_=x8_raw[:].rearrange("p j d -> p d j"))
+        x8_codes = pool.tile([P, D], U32, name="x8_codes", align_bytes=64)
+        x8_scales = pool.tile([P, D], U8, name="x8_scales", align_bytes=64)
+        nc.vector.quantize_mx(
+            out=x8_codes[:].bitcast(E4M3), scales=x8_scales[:], in_=x8_grp[:].rearrange("p d j -> p (d j)")
+        )
+
+        for g, raw, start in ((2, raw2, True), (0, raw0, False)):
+            interleave(g, 0, raw, 0, 256)
+            interleave(g, 1, raw, N, 256)
+            quantize(g, 0)
+            multiply(g, 0, start, False)
+            interleave(g, 2, raw, 2 * N, 256)
+            quantize(g, 1)
+            multiply(g, 1, start, False)
+            quantize(g, 2)
+            multiply(g, 2, start, False)
+
+        interleave(1, 0, raw1a, 0, 512)
+        interleave(1, 1, raw1a, N, 32)
+        quantize(1, 0)
+        multiply(1, 0, False, True)
+        quantize(1, 1)
+        multiply(1, 1, False, True)
+        interleave(1, 2, raw1b, 0, 128)
+        finish(0, 0)
+        finish(0, 1)
+        quantize(1, 2)
+        multiply(1, 2, False, True)
+        finish(1, 0)
+        finish(1, 1)
+        finish(2, 0)
+        finish(2, 1, parts=2)

@@ -14,10 +14,12 @@ E5M2 = mybir.dt.float8_e5m2_x4
 E2M1 = mybir.dt.float4_e2m1fn_x4
 MULT = mybir.AluOpType.mult
 ADD = mybir.AluOpType.add
+COPY = mybir.ActivationFunctionType.Copy
 
 P = 128
 N = 512
 T, D, H = 1536, 256, 1536
+BULK = (320, 288, 256)
 
 
 def tile_mix_dwsav_sgd_kernel(tc, x4_words, x4_scales, x8, dy, w, out):
@@ -32,57 +34,53 @@ def tile_mix_dwsav_sgd_kernel(tc, x4_words, x4_scales, x8, dy, w, out):
             for m in range(2):
                 acc[c, m] = psum.tile([P, N], F32, name="acc_%d_%d" % (c, m))
 
+        raw = {}
+
         def load_dy(g, lo, hi):
-            raw = pool.tile([P, 4, hi - lo], F32, name="raw_%d_%d" % (g, lo), align_bytes=64)
+            t = pool.tile([P, 4, hi - lo], F32, name="raw_%d_%d" % (g, lo), align_bytes=64)
             rows = dy[512 * g : 512 * (g + 1), lo:hi]
-            nc.sync.dma_start(out=raw[:], in_=rows.rearrange("(p j) h -> p j h", j=4))
-            return raw
+            nc.sync.dma_start(out=t[:], in_=rows.rearrange("(p j) h -> p j h", j=4))
+            for h in range(lo, hi):
+                raw[g, h] = (t, lo)
 
-        x4_sc = pool.tile([P, 2, D], U8, name="x4_sc", align_bytes=64)
-        nc.vector.memset(x4_sc[:].rearrange("p a n -> p (a n)").bitcast(I32), 0)
-
-        x8_raw = pool.tile([P, 4, D], F32, name="x8_raw", align_bytes=64)
-        nc.sync.dma_start(out=x8_raw[:], in_=x8.rearrange("(p j) d -> p j d", j=4))
-        x4_wd = pool.tile([P, 2, 2 * D], U8, name="x4_wd", align_bytes=64)
-        nc.sync.dma_start(out=x4_wd[:].bitcast(I32), in_=x4_words.rearrange("a p b -> p a b").bitcast(I32))
-        raw2 = load_dy(2, 0, H)
-        for q in range(4):
-            nc.scalar.dma_start(
-                out=x4_sc[32 * q : 32 * q + 4, :, :].bitcast(I32),
-                in_=x4_scales[:, 4 * q : 4 * q + 4, :].rearrange("a r n -> r a n").bitcast(I32),
-            )
-        raw0 = load_dy(0, 0, H)
-        raw1a = load_dy(1, 0, 2 * N)
-        raw1b = load_dy(1, 2 * N, H)
         w_sb = {}
-        for c in range(3):
-            for m in range(2):
-                w_sb[c, m] = pool.tile([P, N], F32, name="w_%d_%d" % (c, m), align_bytes=64)
-                nc.sync.dma_start(out=w_sb[c, m][:], in_=w[P * m : P * (m + 1), N * c : N * (c + 1)])
+
+        def load_w(m, lo, hi):
+            t = pool.tile([P, hi - lo], F32, name="w_%d_%d" % (m, lo), align_bytes=64)
+            nc.sync.dma_start(out=t[:], in_=w[P * m : P * (m + 1), lo:hi])
+            for h in range(lo, hi):
+                w_sb[m, h] = (t, lo)
 
         grouped, codes, scales = {}, {}, {}
+        for g in range(3):
+            for c in range(3):
+                codes[g, c] = pool.tile([P, N], U32, name="cod_%d_%d" % (g, c), align_bytes=64)
+                scales[g, c] = pool.tile([P, N], U8, name="sca_%d_%d" % (g, c), align_bytes=64)
 
-        def interleave(g, c, raw, col, v):
-            t = pool.tile([P, N, 4], BF16, name="grp_%d_%d" % (g, c), align_bytes=64)
-            grouped[g, c] = t
-            if v < N:
-                nc.scalar.copy(
-                    out=t[:, v:N, :].rearrange("p (c i) j -> p c j i", i=4),
-                    in_=raw[:, :, col + v : col + N].rearrange("p j (c i) -> p c j i", i=4),
-                )
-            if v > 0:
-                nc.vector.tensor_copy(
-                    out=t[:, 0:v, :].rearrange("p (c i) j -> p c j i", i=4),
-                    in_=raw[:, :, col : col + v].rearrange("p j (c i) -> p c j i", i=4),
-                )
+        def stage(g, lo, hi):
+            t = pool.tile([P, hi - lo, 4], BF16, name="grp_%d_%d" % (g, lo), align_bytes=64)
+            for h in range(lo, hi):
+                grouped[g, h] = (t, lo)
 
-        def quantize(g, c):
-            k = pool.tile([P, N], U32, name="cod_%d_%d" % (g, c), align_bytes=64)
-            s = pool.tile([P, N], U8, name="sca_%d_%d" % (g, c), align_bytes=64)
+        def copy(engine, g, lo, hi):
+            src, s0 = raw[g, lo]
+            dst, d0 = grouped[g, lo]
+            o = dst[:, lo - d0 : hi - d0, :].rearrange("p (c i) j -> p c j i", i=4)
+            i = src[:, :, lo - s0 : hi - s0].rearrange("p j (c i) -> p c j i", i=4)
+            if engine == "S":
+                nc.scalar.copy(out=o, in_=i)
+            else:
+                nc.vector.tensor_copy(out=o, in_=i)
+
+        def quantize(g, lo, hi):
+            src, s0 = grouped[g, lo]
+            c = lo // N
+            cols = slice(lo - N * c, hi - N * c)
             nc.vector.quantize_mx(
-                out=k[:].bitcast(E5M2), scales=s[:], in_=grouped[g, c][:].rearrange("p h j -> p (h j)")
+                out=codes[g, c][:, cols].bitcast(E5M2),
+                scales=scales[g, c][:, cols],
+                in_=src[:, lo - s0 : hi - s0, :].rearrange("p h j -> p (h j)"),
             )
-            codes[g, c], scales[g, c] = k, s
 
         def multiply(g, c, start, stop):
             for m in range(2):
@@ -105,13 +103,62 @@ def tile_mix_dwsav_sgd_kernel(tc, x4_words, x4_scales, x8, dy, w, out):
         def finish(c, m, parts=1):
             width = N // parts
             for i in range(parts):
-                cols = slice(width * i, width * (i + 1))
+                h0 = N * c + width * i
+                wt, w0 = w_sb[m, h0]
                 o = pool.tile([P, width], F32, name="o_%d_%d_%d" % (c, m, i), align_bytes=64)
                 nc.vector.scalar_tensor_tensor(
-                    out=o[:], in0=acc[c, m][:, cols], scalar=-0.0625, in1=w_sb[c, m][:, cols], op0=MULT, op1=ADD
+                    out=o[:],
+                    in0=acc[c, m][:, width * i : width * (i + 1)],
+                    scalar=-0.0625,
+                    in1=wt[:, h0 - w0 : h0 - w0 + width],
+                    op0=MULT,
+                    op1=ADD,
                 )
-                h0 = N * c + width * i
                 nc.sync.dma_start(out=out[P * m : P * (m + 1), h0 : h0 + width], in_=o[:])
+
+        scaled, o_tiles = {}, {}
+
+        def prescale(c, m, split):
+            t = pool.tile([P, N - split], F32, name="y_%d_%d" % (c, m), align_bytes=64)
+            nc.scalar.activation(out=t[:], in_=acc[c, m][:, split:N], func=COPY, scale=-0.0625)
+            scaled[c, m] = t
+
+        def finish_shared(c, m, split):
+            h0 = N * c
+            wt, w0 = w_sb[m, h0]
+            o = pool.tile([P, N], F32, name="o_%d_%d" % (c, m), align_bytes=64)
+            nc.gpsimd.tensor_tensor(
+                out=o[:, split:N], in0=scaled[c, m][:], in1=wt[:, h0 - w0 + split : h0 - w0 + N], op=ADD
+            )
+            nc.vector.scalar_tensor_tensor(
+                out=o[:, 0:split],
+                in0=acc[c, m][:, 0:split],
+                scalar=-0.0625,
+                in1=wt[:, h0 - w0 : h0 - w0 + split],
+                op0=MULT,
+                op1=ADD,
+            )
+            nc.sync.dma_start(out=out[P * m : P * (m + 1), h0 : h0 + N], in_=o[:])
+
+        x4_sc = pool.tile([P, 2, D], U8, name="x4_sc", align_bytes=64)
+        nc.vector.memset(x4_sc[:].rearrange("p a n -> p (a n)").bitcast(I32), 0)
+
+        x8_raw = pool.tile([P, 4, D], F32, name="x8_raw", align_bytes=64)
+        nc.sync.dma_start(out=x8_raw[:], in_=x8.rearrange("(p j) d -> p j d", j=4))
+        x4_wd = pool.tile([P, 2, 2 * D], U8, name="x4_wd", align_bytes=64)
+        nc.sync.dma_start(out=x4_wd[:].bitcast(I32), in_=x4_words.rearrange("a p b -> p a b").bitcast(I32))
+        load_dy(2, 0, H)
+        for q in range(4):
+            nc.scalar.dma_start(
+                out=x4_sc[32 * q : 32 * q + 4, :, :].bitcast(I32),
+                in_=x4_scales[:, 4 * q : 4 * q + 4, :].rearrange("a r n -> r a n").bitcast(I32),
+            )
+        load_dy(0, 0, H)
+        load_dy(1, 0, 2 * N)
+        load_dy(1, 2 * N, H)
+        for c in range(3):
+            for m in range(2):
+                load_w(m, N * c, N * (c + 1))
 
         x8_grp = pool.tile([P, D, 4], BF16, name="x8_grp", align_bytes=64)
         nc.scalar.copy(out=x8_grp[:], in_=x8_raw[:].rearrange("p j d -> p d j"))
@@ -121,29 +168,38 @@ def tile_mix_dwsav_sgd_kernel(tc, x4_words, x4_scales, x8, dy, w, out):
             out=x8_codes[:].bitcast(E4M3), scales=x8_scales[:], in_=x8_grp[:].rearrange("p d j -> p (d j)")
         )
 
-        for g, raw, start in ((2, raw2, True), (0, raw0, False)):
-            interleave(g, 0, raw, 0, 256)
-            interleave(g, 1, raw, N, 256)
-            quantize(g, 0)
+        for g, start in ((2, True), (0, False)):
+            for c in range(3):
+                stage(g, N * c, N * (c + 1))
+            for c in range(3):
+                copy("S", g, N * c + BULK[c], N * (c + 1))
+            copy("V", g, 0, BULK[0])
+            copy("V", g, N, N + BULK[1])
+            quantize(g, 0, N)
             multiply(g, 0, start, False)
-            interleave(g, 2, raw, 2 * N, 256)
-            quantize(g, 1)
+            copy("V", g, 2 * N, 2 * N + BULK[2])
+            quantize(g, N, 2 * N)
             multiply(g, 1, start, False)
-            quantize(g, 2)
+            quantize(g, 2 * N, 3 * N)
             multiply(g, 2, start, False)
 
-        interleave(1, 0, raw1a, 0, 512)
-        interleave(1, 1, raw1a, N, 32)
-        quantize(1, 0)
+        for c in range(3):
+            stage(1, N * c, N * (c + 1))
+        copy("S", 1, N + 96, 2 * N)
+        copy("V", 1, 0, N)
+        copy("V", 1, N, N + 96)
+        quantize(1, 0, N)
         multiply(1, 0, False, True)
-        quantize(1, 1)
+        quantize(1, N, 2 * N)
         multiply(1, 1, False, True)
-        interleave(1, 2, raw1b, 0, 128)
+        copy("S", 1, 2 * N + 160, H)
+        copy("V", 1, 2 * N, 2 * N + 160)
+        prescale(1, 0, 384)
         finish(0, 0)
         finish(0, 1)
-        quantize(1, 2)
+        quantize(1, 2 * N, H)
         multiply(1, 2, False, True)
-        finish(1, 0)
+        finish_shared(1, 0, 384)
         finish(1, 1)
         finish(2, 0)
-        finish(2, 1, parts=2)
+        finish(2, 1)

@@ -65,8 +65,8 @@ def tile_mix_dwsav_sgd_kernel(tc, x4_words, x4_scales, x8, dy, w, out):
         def copy(engine, g, lo, hi):
             src, s0 = raw[g, lo]
             dst, d0 = grouped[g, lo]
-            o = dst[:, lo - d0 : hi - d0, :].rearrange("p (c i) j -> p c j i", i=4)
-            i = src[:, :, lo - s0 : hi - s0].rearrange("p j (c i) -> p c j i", i=4)
+            o = dst[:, lo - d0 : hi - d0, :].rearrange("p (c i) j -> p c j i", i=2)
+            i = src[:, :, lo - s0 : hi - s0].rearrange("p j (c i) -> p c j i", i=2)
             if engine == "S":
                 nc.scalar.copy(out=o, in_=i)
             else:

@@ -68,6 +68,8 @@ def tile_mix_dwsav_sgd_kernel(tc, x4_words, x4_scales, x8, dy, w, out):
             o = dst[:, lo - d0 : hi - d0, :].rearrange("p (c i) j -> p c j i", i=2)
             i = src[:, :, lo - s0 : hi - s0].rearrange("p j (c i) -> p c j i", i=2)
             if engine == "S":
+                o = dst[:, lo - d0 : hi - d0, :].rearrange("p (c i) (a b) -> p c a i b", i=8, a=2)
+                i = src[:, :, lo - s0 : hi - s0].rearrange("p (a b) (c i) -> p c a i b", i=8, a=2)
                 nc.scalar.copy(out=o, in_=i)
             else:
                 nc.vector.tensor_copy(out=o, in_=i)

@@ -194,8 +194,8 @@ def tile_mix_dwsav_sgd_kernel(tc, x4_words, x4_scales, x8, dy, w, out):
         multiply(1, 0, False, True)
         quantize(1, N, 2 * N)
         multiply(1, 1, False, True)
-        copy("S", 1, 2 * N + 160, H)
-        copy("V", 1, 2 * N, 2 * N + 160)
+        copy("S", 1, 2 * N + 192, H)
+        copy("V", 1, 2 * N, 2 * N + 192)
         prescale(1, 0, 384)
         finish(0, 0)
         finish(0, 1)

@@ -18,8 +18,13 @@ COPY = mybir.ActivationFunctionType.Copy
 
 P = 128
 N = 512
-T, D, H = 1536, 256, 1536
-BULK = (320, 288, 256)
+D, H = 256, 1536
+ALIGN = 256
+STEP = -0.0625
+WHOLE_SHARE = (320, 288, 256)
+LAST_SHARE = (336, 320, 192)
+HALF = N // 2
+VECTOR_PART = 384
 
 
 def tile_mix_dwsav_sgd_kernel(tc, x4_words, x4_scales, x8, dy, w, out):
@@ -29,59 +34,70 @@ def tile_mix_dwsav_sgd_kernel(tc, x4_words, x4_scales, x8, dy, w, out):
         psum = ctx.enter_context(tc.psum_pool(name="psum", bufs=1))
         ctx.enter_context(tc.manual_schedule())
 
-        acc = {}
+        def sbuf(name, shape, dtype):
+            return pool.tile(shape, dtype, name=name, align_bytes=ALIGN)
+
+        acc, raw, grouped, codes, scales, w_sb, x4_wd = {}, {}, {}, {}, {}, {}, {}
         for c in range(3):
             for m in range(2):
                 acc[c, m] = psum.tile([P, N], F32, name="acc_%d_%d" % (c, m))
+            for g in range(3):
+                grouped[g, c] = sbuf("grp_%d_%d" % (g, c), [P, N, 4], BF16)
+                codes[g, c] = sbuf("cod_%d_%d" % (g, c), [P, N], U32)
+                scales[g, c] = sbuf("sca_%d_%d" % (g, c), [P, N], U8)
 
-        raw = {}
+        def rows_of(g):
+            return dy[512 * g : 512 * (g + 1), :].rearrange("(p j) h -> p j h", j=4)
 
-        def load_dy(g, lo, hi):
-            t = pool.tile([P, 4, hi - lo], F32, name="raw_%d_%d" % (g, lo), align_bytes=64)
-            rows = dy[512 * g : 512 * (g + 1), lo:hi]
-            nc.sync.dma_start(out=t[:], in_=rows.rearrange("(p j) h -> p j h", j=4))
-            for h in range(lo, hi):
-                raw[g, h] = (t, lo)
+        def pairs(t, pitch, c):
+            view = t[:, 0 : 2 * pitch * H].rearrange("p (a r h) -> p a r h", a=2, r=pitch)
+            return view[:, :, 0:2, N * c : N * (c + 1)]
 
-        w_sb = {}
+        def load_x4_words(g):
+            x4_wd[g] = sbuf("x4_wd_%d" % g, [P, 2 * D], U8)
+            nc.sync.dma_start(out=x4_wd[g][:].bitcast(I32), in_=x4_words[g].bitcast(I32))
 
-        def load_w(m, lo, hi):
-            t = pool.tile([P, hi - lo], F32, name="w_%d_%d" % (m, lo), align_bytes=64)
-            nc.sync.dma_start(out=t[:], in_=w[P * m : P * (m + 1), lo:hi])
-            for h in range(lo, hi):
-                w_sb[m, h] = (t, lo)
-
-        grouped, codes, scales = {}, {}, {}
-        for g in range(3):
+        def load_whole(g):
+            t = sbuf("raw_%d" % g, [P, 4 * H], F32)
+            nc.sync.dma_start(out=t[:], in_=rows_of(g).rearrange("p j h -> p (j h)"))
             for c in range(3):
-                codes[g, c] = pool.tile([P, N], U32, name="cod_%d_%d" % (g, c), align_bytes=64)
-                scales[g, c] = pool.tile([P, N], U8, name="sca_%d_%d" % (g, c), align_bytes=64)
+                raw[g, c] = pairs(t, 2, c)
 
-        def stage(g, lo, hi):
-            t = pool.tile([P, hi - lo, 4], BF16, name="grp_%d_%d" % (g, lo), align_bytes=64)
-            for h in range(lo, hi):
-                grouped[g, h] = (t, lo)
+        def load_staircase(g):
+            t = sbuf("raw_%d" % g, [P, 24 * N], F32)
+            first = t[:, 0 : 8 * N].rearrange("p (a x) -> p a x", a=2)
+            raw[g, 0] = first.rearrange("p a (k n) -> p a k n", n=N)[:, :, 0:4:3, :]
+            for c in (1, 2):
+                view = t[:, 0 : 8 * (c + 1) * N].rearrange("p (b r k n) -> p r b k n", b=2, k=4, n=N)
+                raw[g, c] = view[:, 0:2, :, c, :]
+            by_pair = rows_of(g).rearrange("p (a b) h -> p a (b h)", a=2)
+            nc.sync.dma_start(out=first, in_=by_pair[:, :, 0 : H + N])
+            for c in (1, 2):
+                if c == 2:
+                    load_x4_words(g)
+                nc.sync.dma_start(out=raw[g, c][:, :, 1, :], in_=by_pair[:, :, H + N * c : H + N * (c + 1)])
 
-        def copy(engine, g, lo, hi):
-            src, s0 = raw[g, lo]
-            dst, d0 = grouped[g, lo]
-            o = dst[:, lo - d0 : hi - d0, :].rearrange("p (c i) j -> p c j i", i=2)
-            i = src[:, :, lo - s0 : hi - s0].rearrange("p j (c i) -> p c j i", i=2)
-            if engine == "S":
-                o = dst[:, lo - d0 : hi - d0, :].rearrange("p (c i) (a b) -> p c a i b", i=8, a=2)
-                i = src[:, :, lo - s0 : hi - s0].rearrange("p (a b) (c i) -> p c a i b", i=8, a=2)
-                nc.scalar.copy(out=o, in_=i)
-            else:
-                nc.vector.tensor_copy(out=o, in_=i)
+        def load_w(c, m):
+            w_sb[c, m] = sbuf("w_%d_%d" % (c, m), [P, N], F32)
+            nc.sync.dma_start(out=w_sb[c, m][:], in_=w[P * m : P * (m + 1), N * c : N * (c + 1)])
 
-        def quantize(g, lo, hi):
-            src, s0 = grouped[g, lo]
-            c = lo // N
-            cols = slice(lo - N * c, hi - N * c)
+        def interleave_vector(g, c, hi, lo=0):
+            nc.vector.tensor_copy(
+                out=grouped[g, c][:, lo:hi, :].rearrange("p (n i) (a b) -> p n a b i", i=2, a=2),
+                in_=raw[g, c][:, :, :, lo:hi].rearrange("p a b (n i) -> p n a b i", i=2),
+            )
+
+        def interleave_scalar(g, c, share):
+            nc.scalar.copy(
+                out=grouped[g, c][:, share:N, :].rearrange("p (n i) (a b) -> p n a i b", i=8, a=2),
+                in_=raw[g, c][:, :, :, share:N].rearrange("p a b (n i) -> p n a i b", i=8),
+            )
+
+        def quantize(g, c, lo=0, hi=N):
             nc.vector.quantize_mx(
-                out=codes[g, c][:, cols].bitcast(E5M2),
-                scales=scales[g, c][:, cols],
-                in_=src[:, lo - s0 : hi - s0, :].rearrange("p h j -> p (h j)"),
+                out=codes[g, c][:, lo:hi].bitcast(E5M2),
+                scales=scales[g, c][:, lo:hi],
+                in_=grouped[g, c][:, lo:hi, :].rearrange("p h j -> p (h j)"),
             )
 
         def multiply(g, c, start, stop):
@@ -90,7 +106,7 @@ def tile_mix_dwsav_sgd_kernel(tc, x4_words, x4_scales, x8, dy, w, out):
                     lhsT = x8_codes[:, P * m : P * (m + 1)].bitcast(E4M3)
                     lhsT_scale = x8_scales[:, P * m : P * (m + 1)]
                 else:
-                    lhsT = x4_wd[:, g, 2 * P * m : 2 * P * (m + 1)].bitcast(E2M1)
+                    lhsT = x4_wd[g][:, 2 * P * m : 2 * P * (m + 1)].bitcast(E2M1)
                     lhsT_scale = x4_sc[:, g, P * m : P * (m + 1)]
                 nc.tensor.matmul_mx(
                     out=acc[c, m][:],
@@ -102,106 +118,82 @@ def tile_mix_dwsav_sgd_kernel(tc, x4_words, x4_scales, x8, dy, w, out):
                     stop=stop,
                 )
 
-        def finish(c, m, parts=1):
-            width = N // parts
-            for i in range(parts):
-                h0 = N * c + width * i
-                wt, w0 = w_sb[m, h0]
-                o = pool.tile([P, width], F32, name="o_%d_%d_%d" % (c, m, i), align_bytes=64)
-                nc.vector.scalar_tensor_tensor(
-                    out=o[:],
-                    in0=acc[c, m][:, width * i : width * (i + 1)],
-                    scalar=-0.0625,
-                    in1=wt[:, h0 - w0 : h0 - w0 + width],
-                    op0=MULT,
-                    op1=ADD,
-                )
-                nc.sync.dma_start(out=out[P * m : P * (m + 1), h0 : h0 + width], in_=o[:])
+        scaled = {}
 
-        scaled, o_tiles = {}, {}
+        def prescale(c, m):
+            scaled[c, m] = sbuf("y_%d_%d" % (c, m), [P, N - VECTOR_PART], F32)
+            nc.scalar.activation(out=scaled[c, m][:], in_=acc[c, m][:, VECTOR_PART:N], func=COPY, scale=STEP)
 
-        def prescale(c, m, split):
-            t = pool.tile([P, N - split], F32, name="y_%d_%d" % (c, m), align_bytes=64)
-            nc.scalar.activation(out=t[:], in_=acc[c, m][:, split:N], func=COPY, scale=-0.0625)
-            scaled[c, m] = t
-
-        def finish_shared(c, m, split):
-            h0 = N * c
-            wt, w0 = w_sb[m, h0]
-            o = pool.tile([P, N], F32, name="o_%d_%d" % (c, m), align_bytes=64)
-            nc.gpsimd.tensor_tensor(
-                out=o[:, split:N], in0=scaled[c, m][:], in1=wt[:, h0 - w0 + split : h0 - w0 + N], op=ADD
-            )
+        def finish(c, m):
+            o = sbuf("o_%d_%d" % (c, m), [P, N], F32)
+            part = N
+            if (c, m) in scaled:
+                part = VECTOR_PART
+                nc.gpsimd.tensor_tensor(out=o[:, part:N], in0=scaled[c, m][:], in1=w_sb[c, m][:, part:N], op=ADD)
             nc.vector.scalar_tensor_tensor(
-                out=o[:, 0:split],
-                in0=acc[c, m][:, 0:split],
-                scalar=-0.0625,
-                in1=wt[:, h0 - w0 : h0 - w0 + split],
+                out=o[:, 0:part],
+                in0=acc[c, m][:, 0:part],
+                scalar=STEP,
+                in1=w_sb[c, m][:, 0:part],
                 op0=MULT,
                 op1=ADD,
             )
-            nc.sync.dma_start(out=out[P * m : P * (m + 1), h0 : h0 + N], in_=o[:])
+            nc.sync.dma_start(out=out[P * m : P * (m + 1), N * c : N * (c + 1)], in_=o[:])
 
-        x4_sc = pool.tile([P, 2, D], U8, name="x4_sc", align_bytes=64)
+        x4_sc = sbuf("x4_sc", [P, 2, D], U8)
         nc.vector.memset(x4_sc[:].rearrange("p a n -> p (a n)").bitcast(I32), 0)
 
-        x8_raw = pool.tile([P, 4, D], F32, name="x8_raw", align_bytes=64)
+        x8_raw = sbuf("x8_raw", [P, 4, D], F32)
         nc.sync.dma_start(out=x8_raw[:], in_=x8.rearrange("(p j) d -> p j d", j=4))
-        x4_wd = pool.tile([P, 2, 2 * D], U8, name="x4_wd", align_bytes=64)
-        nc.sync.dma_start(out=x4_wd[:].bitcast(I32), in_=x4_words.rearrange("a p b -> p a b").bitcast(I32))
-        load_dy(2, 0, H)
+        load_x4_words(0)
+        load_whole(2)
         for q in range(4):
             nc.scalar.dma_start(
                 out=x4_sc[32 * q : 32 * q + 4, :, :].bitcast(I32),
                 in_=x4_scales[:, 4 * q : 4 * q + 4, :].rearrange("a r n -> r a n").bitcast(I32),
             )
-        load_dy(0, 0, H)
-        load_dy(1, 0, 2 * N)
-        load_dy(1, 2 * N, H)
+        load_whole(0)
+        load_staircase(1)
         for c in range(3):
             for m in range(2):
-                load_w(m, N * c, N * (c + 1))
+                load_w(c, m)
 
-        x8_grp = pool.tile([P, D, 4], BF16, name="x8_grp", align_bytes=64)
+        x8_grp = sbuf("x8_grp", [P, D, 4], BF16)
         nc.scalar.copy(out=x8_grp[:], in_=x8_raw[:].rearrange("p j d -> p d j"))
-        x8_codes = pool.tile([P, D], U32, name="x8_codes", align_bytes=64)
-        x8_scales = pool.tile([P, D], U8, name="x8_scales", align_bytes=64)
+        x8_codes = sbuf("x8_codes", [P, D], U32)
+        x8_scales = sbuf("x8_scales", [P, D], U8)
         nc.vector.quantize_mx(
             out=x8_codes[:].bitcast(E4M3), scales=x8_scales[:], in_=x8_grp[:].rearrange("p d j -> p (d j)")
         )
 
         for g, start in ((2, True), (0, False)):
             for c in range(3):
-                stage(g, N * c, N * (c + 1))
-            for c in range(3):
-                copy("S", g, N * c + BULK[c], N * (c + 1))
-            copy("V", g, 0, BULK[0])
-            copy("V", g, N, N + BULK[1])
-            quantize(g, 0, N)
+                interleave_scalar(g, c, WHOLE_SHARE[c])
+            interleave_vector(g, 0, WHOLE_SHARE[0])
+            interleave_vector(g, 1, WHOLE_SHARE[1])
+            quantize(g, 0)
             multiply(g, 0, start, False)
-            copy("V", g, 2 * N, 2 * N + BULK[2])
-            quantize(g, N, 2 * N)
+            interleave_vector(g, 2, WHOLE_SHARE[2])
+            quantize(g, 1)
             multiply(g, 1, start, False)
-            quantize(g, 2 * N, 3 * N)
+            quantize(g, 2)
             multiply(g, 2, start, False)
 
-        for c in range(3):
-            stage(1, N * c, N * (c + 1))
-        copy("S", 1, N + 96, 2 * N)
-        copy("V", 1, 0, N)
-        copy("V", 1, N, N + 96)
-        quantize(1, 0, N)
-        multiply(1, 0, False, True)
-        quantize(1, N, 2 * N)
-        multiply(1, 1, False, True)
-        copy("S", 1, 2 * N + 192, H)
-        copy("V", 1, 2 * N, 2 * N + 192)
-        prescale(1, 0, 384)
+        for c in range(2):
+            interleave_scalar(1, c, LAST_SHARE[c])
+            interleave_vector(1, c, HALF)
+            interleave_vector(1, c, LAST_SHARE[c], HALF)
+            quantize(1, c, 0, HALF)
+            quantize(1, c, HALF, N)
+            multiply(1, c, False, True)
+        interleave_scalar(1, 2, LAST_SHARE[2])
+        interleave_vector(1, 2, LAST_SHARE[2])
+        prescale(1, 0)
         finish(0, 0)
         finish(0, 1)
-        quantize(1, 2 * N, H)
+        quantize(1, 2)
         multiply(1, 2, False, True)
-        finish_shared(1, 0, 384)
+        finish(1, 0)
         finish(1, 1)
         finish(2, 0)
         finish(2, 1)

@@ -189,6 +189,7 @@ def tile_mix_dwsav_sgd_kernel(tc, x4_words, x4_scales, x8, dy, w, out):
         interleave_scalar(1, 2, LAST_SHARE[2])
         interleave_vector(1, 2, LAST_SHARE[2])
         prescale(1, 0)
+        prescale(1, 1)
         finish(0, 0)
         finish(0, 1)
         quantize(1, 2)

@@ -22,7 +22,7 @@ D, H = 256, 1536
 ALIGN = 256
 STEP = -0.0625
 WHOLE_SHARE = (320, 288, 256)
-LAST_SHARE = (336, 320, 192)
+LAST_SHARE = (304, 256, 192)
 HALF = N // 2
 VECTOR_PART = 384
 
@@ -179,15 +179,18 @@ def tile_mix_dwsav_sgd_kernel(tc, x4_words, x4_scales, x8, dy, w, out):
             quantize(g, 2)
             multiply(g, 2, start, False)
 
-        for c in range(2):
+        for c in range(3):
             interleave_scalar(1, c, LAST_SHARE[c])
-            interleave_vector(1, c, HALF)
-            interleave_vector(1, c, LAST_SHARE[c], HALF)
-            quantize(1, c, 0, HALF)
-            quantize(1, c, HALF, N)
-            multiply(1, c, False, True)
-        interleave_scalar(1, 2, LAST_SHARE[2])
+        interleave_vector(1, 0, HALF)
+        interleave_vector(1, 0, LAST_SHARE[0], HALF)
+        quantize(1, 0, 0, HALF)
+        interleave_vector(1, 1, LAST_SHARE[1])
+        quantize(1, 0, HALF, N)
+        multiply(1, 0, False, True)
+        quantize(1, 1, 0, HALF)
         interleave_vector(1, 2, LAST_SHARE[2])
+        quantize(1, 1, HALF, N)
+        multiply(1, 1, False, True)
         prescale(1, 0)
         prescale(1, 1)
         finish(0, 0)

@@ -22,7 +22,7 @@ D, H = 256, 1536
 ALIGN = 256
 STEP = -0.0625
 WHOLE_SHARE = (320, 288, 256)
-LAST_SHARE = (304, 256, 192)
+LAST_SHARE = 208
 HALF = N // 2
 VECTOR_PART = 384
 
@@ -38,13 +38,31 @@ def tile_mix_dwsav_sgd_kernel(tc, x4_words, x4_scales, x8, dy, w, out):
             return pool.tile(shape, dtype, name=name, align_bytes=ALIGN)
 
         acc, raw, grouped, codes, scales, w_sb, x4_wd = {}, {}, {}, {}, {}, {}, {}
+        banks = {0: ((0, N),), 1: ((0, N),), 2: ((0, HALF), (HALF, N))}
         for c in range(3):
-            for m in range(2):
-                acc[c, m] = psum.tile([P, N], F32, name="acc_%d_%d" % (c, m))
+            for lo, hi in banks[c]:
+                for m in range(2):
+                    bank = psum.tile([P, N], F32, name="acc_%d_%d_%d" % (c, lo, m))
+                    acc[c, lo, m] = bank[:, 0 : hi - lo]
             for g in range(3):
-                grouped[g, c] = sbuf("grp_%d_%d" % (g, c), [P, N, 4], BF16)
+                if (g, c) != (1, 2):
+                    grouped[g, c] = sbuf("grp_%d_%d" % (g, c), [P, N, 4], BF16)
                 codes[g, c] = sbuf("cod_%d_%d" % (g, c), [P, N], U32)
                 scales[g, c] = sbuf("sca_%d_%d" % (g, c), [P, N], U8)
+
+        result, last_half = {}, {}
+        for tile, lo in (((0, 1), 0), ((1, 1), HALF)):
+            both = sbuf("both_%d" % lo, [P, VECTOR_PART + 2 * HALF], F32)
+            result[tile] = both[:, 0:N]
+            last_half[lo] = both[:, VECTOR_PART:].bitcast(BF16).rearrange("p (h j) -> p h j", j=4)
+        for tile in ((0, 0), (1, 0), (2, 0), (2, 1)):
+            result[tile] = sbuf("o_%d_%d" % tile, [P, N], F32)[:]
+
+        def interleaved(g, c, lo, hi):
+            if (g, c) != (1, 2):
+                return grouped[g, c][:, lo:hi, :]
+            base = lo // HALF * HALF
+            return last_half[base][:, lo - base : hi - base, :]
 
         def rows_of(g):
             return dy[512 * g : 512 * (g + 1), :].rearrange("(p j) h -> p j h", j=4)
@@ -83,24 +101,28 @@ def tile_mix_dwsav_sgd_kernel(tc, x4_words, x4_scales, x8, dy, w, out):
 
         def interleave_vector(g, c, hi, lo=0):
             nc.vector.tensor_copy(
-                out=grouped[g, c][:, lo:hi, :].rearrange("p (n i) (a b) -> p n a b i", i=2, a=2),
+                out=interleaved(g, c, lo, hi).rearrange("p (n i) (a b) -> p n a b i", i=2, a=2),
                 in_=raw[g, c][:, :, :, lo:hi].rearrange("p a b (n i) -> p n a b i", i=2),
             )
 
-        def interleave_scalar(g, c, share):
+        def interleave_scalar(g, c, lo, hi=N):
             nc.scalar.copy(
-                out=grouped[g, c][:, share:N, :].rearrange("p (n i) (a b) -> p n a i b", i=8, a=2),
-                in_=raw[g, c][:, :, :, share:N].rearrange("p a b (n i) -> p n a i b", i=8),
+                out=interleaved(g, c, lo, hi).rearrange("p (n i) (a b) -> p n a i b", i=8, a=2),
+                in_=raw[g, c][:, :, :, lo:hi].rearrange("p a b (n i) -> p n a i b", i=8),
             )
 
         def quantize(g, c, lo=0, hi=N):
             nc.vector.quantize_mx(
                 out=codes[g, c][:, lo:hi].bitcast(E5M2),
                 scales=scales[g, c][:, lo:hi],
-                in_=grouped[g, c][:, lo:hi, :].rearrange("p h j -> p (h j)"),
+                in_=interleaved(g, c, lo, hi).rearrange("p h j -> p (h j)"),
             )
 
         def multiply(g, c, start, stop):
+            for lo, hi in banks[c]:
+                multiply_bank(g, c, lo, hi, start, stop)
+
+        def multiply_bank(g, c, lo, hi, start, stop):
             for m in range(2):
                 if g == 2:
                     lhsT = x8_codes[:, P * m : P * (m + 1)].bitcast(E4M3)
@@ -109,11 +131,11 @@ def tile_mix_dwsav_sgd_kernel(tc, x4_words, x4_scales, x8, dy, w, out):
                     lhsT = x4_wd[g][:, 2 * P * m : 2 * P * (m + 1)].bitcast(E2M1)
                     lhsT_scale = x4_sc[:, g, P * m : P * (m + 1)]
                 nc.tensor.matmul_mx(
-                    out=acc[c, m][:],
+                    out=acc[c, lo, m],
                     lhsT=lhsT,
                     lhsT_scale=lhsT_scale,
-                    rhs=codes[g, c][:].bitcast(E5M2),
-                    rhs_scale=scales[g, c][:],
+                    rhs=codes[g, c][:, lo:hi].bitcast(E5M2),
+                    rhs_scale=scales[g, c][:, lo:hi],
                     start=start,
                     stop=stop,
                 )
@@ -122,23 +144,25 @@ def tile_mix_dwsav_sgd_kernel(tc, x4_words, x4_scales, x8, dy, w, out):
 
         def prescale(c, m):
             scaled[c, m] = sbuf("y_%d_%d" % (c, m), [P, N - VECTOR_PART], F32)
-            nc.scalar.activation(out=scaled[c, m][:], in_=acc[c, m][:, VECTOR_PART:N], func=COPY, scale=STEP)
+            nc.scalar.activation(out=scaled[c, m][:], in_=acc[c, 0, m][:, VECTOR_PART:N], func=COPY, scale=STEP)
 
         def finish(c, m):
-            o = sbuf("o_%d_%d" % (c, m), [P, N], F32)
+            o = result[c, m]
             part = N
             if (c, m) in scaled:
                 part = VECTOR_PART
                 nc.gpsimd.tensor_tensor(out=o[:, part:N], in0=scaled[c, m][:], in1=w_sb[c, m][:, part:N], op=ADD)
-            nc.vector.scalar_tensor_tensor(
-                out=o[:, 0:part],
-                in0=acc[c, m][:, 0:part],
-                scalar=STEP,
-                in1=w_sb[c, m][:, 0:part],
-                op0=MULT,
-                op1=ADD,
-            )
-            nc.sync.dma_start(out=out[P * m : P * (m + 1), N * c : N * (c + 1)], in_=o[:])
+            for lo, hi in banks[c]:
+                hi = min(hi, part)
+                nc.vector.scalar_tensor_tensor(
+                    out=o[:, lo:hi],
+                    in0=acc[c, lo, m][:, 0 : hi - lo],
+                    scalar=STEP,
+                    in1=w_sb[c, m][:, lo:hi],
+                    op0=MULT,
+                    op1=ADD,
+                )
+            nc.sync.dma_start(out=out[P * m : P * (m + 1), N * c : N * (c + 1)], in_=o)
 
         x4_sc = sbuf("x4_sc", [P, 2, D], U8)
         nc.vector.memset(x4_sc[:].rearrange("p a n -> p (a n)").bitcast(I32), 0)
@@ -179,25 +203,30 @@ def tile_mix_dwsav_sgd_kernel(tc, x4_words, x4_scales, x8, dy, w, out):
             quantize(g, 2)
             multiply(g, 2, start, False)
 
-        for c in range(3):
-            interleave_scalar(1, c, LAST_SHARE[c])
+        for c in range(2):
+            interleave_scalar(1, c, HALF)
         interleave_vector(1, 0, HALF)
-        interleave_vector(1, 0, LAST_SHARE[0], HALF)
         quantize(1, 0, 0, HALF)
-        interleave_vector(1, 1, LAST_SHARE[1])
+        interleave_vector(1, 1, HALF)
         quantize(1, 0, HALF, N)
         multiply(1, 0, False, True)
         quantize(1, 1, 0, HALF)
-        interleave_vector(1, 2, LAST_SHARE[2])
         quantize(1, 1, HALF, N)
         multiply(1, 1, False, True)
+        interleave_vector(1, 2, LAST_SHARE)
+        interleave_scalar(1, 2, LAST_SHARE, HALF)
+        interleave_scalar(1, 2, HALF, VECTOR_PART)
+        prescale(0, 1)
+        interleave_scalar(1, 2, VECTOR_PART, N)
         prescale(1, 0)
         prescale(1, 1)
         finish(0, 0)
+        quantize(1, 2, 0, HALF)
+        multiply_bank(1, 2, 0, HALF, False, True)
         finish(0, 1)
-        quantize(1, 2)
-        multiply(1, 2, False, True)
         finish(1, 0)
+        quantize(1, 2, HALF, N)
+        multiply_bank(1, 2, HALF, N, False, True)
         finish(1, 1)
         finish(2, 0)
         finish(2, 1)

@@ -22,9 +22,9 @@ D, H = 256, 1536
 ALIGN = 256
 STEP = -0.0625
 WHOLE_SHARE = (320, 288, 256)
-LAST_SHARE = 208
+LAST_SHARE = (304, 304, 208)
 HALF = N // 2
-VECTOR_PART = 384
+VECTOR_PART = 352
 
 
 def tile_mix_dwsav_sgd_kernel(tc, x4_words, x4_scales, x8, dy, w, out):
@@ -45,24 +45,9 @@ def tile_mix_dwsav_sgd_kernel(tc, x4_words, x4_scales, x8, dy, w, out):
                     bank = psum.tile([P, N], F32, name="acc_%d_%d_%d" % (c, lo, m))
                     acc[c, lo, m] = bank[:, 0 : hi - lo]
             for g in range(3):
-                if (g, c) != (1, 2):
-                    grouped[g, c] = sbuf("grp_%d_%d" % (g, c), [P, N, 4], BF16)
+                grouped[g, c] = sbuf("grp_%d_%d" % (g, c), [P, N, 4], BF16)
                 codes[g, c] = sbuf("cod_%d_%d" % (g, c), [P, N], U32)
                 scales[g, c] = sbuf("sca_%d_%d" % (g, c), [P, N], U8)
-
-        result, last_half = {}, {}
-        for tile, lo in (((0, 1), 0), ((1, 1), HALF)):
-            both = sbuf("both_%d" % lo, [P, VECTOR_PART + 2 * HALF], F32)
-            result[tile] = both[:, 0:N]
-            last_half[lo] = both[:, VECTOR_PART:].bitcast(BF16).rearrange("p (h j) -> p h j", j=4)
-        for tile in ((0, 0), (1, 0), (2, 0), (2, 1)):
-            result[tile] = sbuf("o_%d_%d" % tile, [P, N], F32)[:]
-
-        def interleaved(g, c, lo, hi):
-            if (g, c) != (1, 2):
-                return grouped[g, c][:, lo:hi, :]
-            base = lo // HALF * HALF
-            return last_half[base][:, lo - base : hi - base, :]
 
         def rows_of(g):
             return dy[512 * g : 512 * (g + 1), :].rearrange("(p j) h -> p j h", j=4)
@@ -91,8 +76,7 @@ def tile_mix_dwsav_sgd_kernel(tc, x4_words, x4_scales, x8, dy, w, out):
             by_pair = rows_of(g).rearrange("p (a b) h -> p a (b h)", a=2)
             nc.sync.dma_start(out=first, in_=by_pair[:, :, 0 : H + N])
             for c in (1, 2):
-                if c == 2:
-                    load_x4_words(g)
+                load_x4_words(c - 1)
                 nc.sync.dma_start(out=raw[g, c][:, :, 1, :], in_=by_pair[:, :, H + N * c : H + N * (c + 1)])
 
         def load_w(c, m):
@@ -101,13 +85,13 @@ def tile_mix_dwsav_sgd_kernel(tc, x4_words, x4_scales, x8, dy, w, out):
 
         def interleave_vector(g, c, hi, lo=0):
             nc.vector.tensor_copy(
-                out=interleaved(g, c, lo, hi).rearrange("p (n i) (a b) -> p n a b i", i=2, a=2),
+                out=grouped[g, c][:, lo:hi, :].rearrange("p (n i) (a b) -> p n a b i", i=2, a=2),
                 in_=raw[g, c][:, :, :, lo:hi].rearrange("p a b (n i) -> p n a b i", i=2),
             )
 
         def interleave_scalar(g, c, lo, hi=N):
             nc.scalar.copy(
-                out=interleaved(g, c, lo, hi).rearrange("p (n i) (a b) -> p n a i b", i=8, a=2),
+                out=grouped[g, c][:, lo:hi, :].rearrange("p (n i) (a b) -> p n a i b", i=8, a=2),
                 in_=raw[g, c][:, :, :, lo:hi].rearrange("p a b (n i) -> p n a i b", i=8),
             )
 
@@ -115,7 +99,7 @@ def tile_mix_dwsav_sgd_kernel(tc, x4_words, x4_scales, x8, dy, w, out):
             nc.vector.quantize_mx(
                 out=codes[g, c][:, lo:hi].bitcast(E5M2),
                 scales=scales[g, c][:, lo:hi],
-                in_=interleaved(g, c, lo, hi).rearrange("p h j -> p (h j)"),
+                in_=grouped[g, c][:, lo:hi, :].rearrange("p h j -> p (h j)"),
             )
 
         def multiply(g, c, start, stop):
@@ -147,7 +131,7 @@ def tile_mix_dwsav_sgd_kernel(tc, x4_words, x4_scales, x8, dy, w, out):
             nc.scalar.activation(out=scaled[c, m][:], in_=acc[c, 0, m][:, VECTOR_PART:N], func=COPY, scale=STEP)
 
         def finish(c, m):
-            o = result[c, m]
+            o = sbuf("o_%d_%d" % (c, m), [P, N], F32)
             part = N
             if (c, m) in scaled:
                 part = VECTOR_PART
@@ -162,17 +146,16 @@ def tile_mix_dwsav_sgd_kernel(tc, x4_words, x4_scales, x8, dy, w, out):
                     op0=MULT,
                     op1=ADD,
                 )
-            nc.sync.dma_start(out=out[P * m : P * (m + 1), N * c : N * (c + 1)], in_=o)
+            nc.sync.dma_start(out=out[P * m : P * (m + 1), N * c : N * (c + 1)], in_=o[:])
 
         x4_sc = sbuf("x4_sc", [P, 2, D], U8)
         nc.vector.memset(x4_sc[:].rearrange("p a n -> p (a n)").bitcast(I32), 0)
 
         x8_raw = sbuf("x8_raw", [P, 4, D], F32)
         nc.sync.dma_start(out=x8_raw[:], in_=x8.rearrange("(p j) d -> p j d", j=4))
-        load_x4_words(0)
         load_whole(2)
         for q in range(4):
-            nc.scalar.dma_start(
+            nc.sync.dma_start(
                 out=x4_sc[32 * q : 32 * q + 4, :, :].bitcast(I32),
                 in_=x4_scales[:, 4 * q : 4 * q + 4, :].rearrange("a r n -> r a n").bitcast(I32),
             )
@@ -190,36 +173,33 @@ def tile_mix_dwsav_sgd_kernel(tc, x4_words, x4_scales, x8, dy, w, out):
             out=x8_codes[:].bitcast(E4M3), scales=x8_scales[:], in_=x8_grp[:].rearrange("p d j -> p (d j)")
         )
 
-        for g, start in ((2, True), (0, False)):
+        for g in (2, 0):
             for c in range(3):
                 interleave_scalar(g, c, WHOLE_SHARE[c])
             interleave_vector(g, 0, WHOLE_SHARE[0])
             interleave_vector(g, 1, WHOLE_SHARE[1])
             quantize(g, 0)
-            multiply(g, 0, start, False)
             interleave_vector(g, 2, WHOLE_SHARE[2])
             quantize(g, 1)
-            multiply(g, 1, start, False)
             quantize(g, 2)
-            multiply(g, 2, start, False)
+            if g == 2:
+                for c in range(3):
+                    multiply(g, c, True, False)
 
         for c in range(2):
-            interleave_scalar(1, c, HALF)
-        interleave_vector(1, 0, HALF)
-        quantize(1, 0, 0, HALF)
-        interleave_vector(1, 1, HALF)
-        quantize(1, 0, HALF, N)
-        multiply(1, 0, False, True)
-        quantize(1, 1, 0, HALF)
-        quantize(1, 1, HALF, N)
-        multiply(1, 1, False, True)
-        interleave_vector(1, 2, LAST_SHARE)
-        interleave_scalar(1, 2, LAST_SHARE, HALF)
-        interleave_scalar(1, 2, HALF, VECTOR_PART)
-        prescale(0, 1)
-        interleave_scalar(1, 2, VECTOR_PART, N)
+            interleave_scalar(1, c, LAST_SHARE[c])
+        for c in range(2):
+            interleave_vector(1, c, HALF)
+            interleave_vector(1, c, LAST_SHARE[c], HALF)
+            quantize(1, c, 0, HALF)
+            quantize(1, c, HALF, N)
+            multiply(0, c, False, False)
+            multiply(1, c, False, True)
+        multiply(0, 2, False, False)
+        interleave_vector(1, 2, LAST_SHARE[2])
+        interleave_scalar(1, 2, LAST_SHARE[2], HALF)
+        interleave_scalar(1, 2, HALF, N)
         prescale(1, 0)
-        prescale(1, 1)
         finish(0, 0)
         quantize(1, 2, 0, HALF)
         multiply_bank(1, 2, 0, HALF, False, True)

@@ -151,8 +151,6 @@ def tile_mix_dwsav_sgd_kernel(tc, x4_words, x4_scales, x8, dy, w, out):
         x4_sc = sbuf("x4_sc", [P, 2, D], U8)
         nc.vector.memset(x4_sc[:].rearrange("p a n -> p (a n)").bitcast(I32), 0)
 
-        x8_raw = sbuf("x8_raw", [P, 4, D], F32)
-        nc.sync.dma_start(out=x8_raw[:], in_=x8.rearrange("(p j) d -> p j d", j=4))
         load_whole(2)
         for q in range(4):
             nc.sync.dma_start(
@@ -160,31 +158,35 @@ def tile_mix_dwsav_sgd_kernel(tc, x4_words, x4_scales, x8, dy, w, out):
                 in_=x4_scales[:, 4 * q : 4 * q + 4, :].rearrange("a r n -> r a n").bitcast(I32),
             )
         load_whole(0)
+        x8_raw = sbuf("x8_raw", [P, 4, D], F32)
+        nc.sync.dma_start(out=x8_raw[:], in_=x8.rearrange("(p j) d -> p j d", j=4))
         load_staircase(1)
         for c in range(3):
             for m in range(2):
                 load_w(c, m)
 
         x8_grp = sbuf("x8_grp", [P, D, 4], BF16)
-        nc.scalar.copy(out=x8_grp[:], in_=x8_raw[:].rearrange("p j d -> p d j"))
         x8_codes = sbuf("x8_codes", [P, D], U32)
         x8_scales = sbuf("x8_scales", [P, D], U8)
-        nc.vector.quantize_mx(
-            out=x8_codes[:].bitcast(E4M3), scales=x8_scales[:], in_=x8_grp[:].rearrange("p d j -> p (d j)")
-        )
 
         for g in (2, 0):
-            for c in range(3):
-                interleave_scalar(g, c, WHOLE_SHARE[c])
+            interleave_scalar(g, 0, WHOLE_SHARE[0])
+            interleave_scalar(g, 1, WHOLE_SHARE[1])
+            if g == 0:
+                nc.scalar.copy(out=x8_grp[:], in_=x8_raw[:].rearrange("p j d -> p d j"))
+            interleave_scalar(g, 2, WHOLE_SHARE[2])
             interleave_vector(g, 0, WHOLE_SHARE[0])
             interleave_vector(g, 1, WHOLE_SHARE[1])
             quantize(g, 0)
             interleave_vector(g, 2, WHOLE_SHARE[2])
             quantize(g, 1)
+            if g == 0:
+                nc.vector.quantize_mx(
+                    out=x8_codes[:].bitcast(E4M3), scales=x8_scales[:], in_=x8_grp[:].rearrange("p d j -> p (d j)")
+                )
             quantize(g, 2)
-            if g == 2:
-                for c in range(3):
-                    multiply(g, c, True, False)
+        for c in range(2):
+            multiply(2, c, True, False)
 
         for c in range(2):
             interleave_scalar(1, c, LAST_SHARE[c])
@@ -195,6 +197,7 @@ def tile_mix_dwsav_sgd_kernel(tc, x4_words, x4_scales, x8, dy, w, out):
             quantize(1, c, HALF, N)
             multiply(0, c, False, False)
             multiply(1, c, False, True)
+        multiply(2, 2, True, False)
         multiply(0, 2, False, False)
         interleave_vector(1, 2, LAST_SHARE[2])
         interleave_scalar(1, 2, LAST_SHARE[2], HALF)

@@ -25,6 +25,7 @@ WHOLE_SHARE = (320, 288, 256)
 LAST_SHARE = (304, 304, 208)
 HALF = N // 2
 VECTOR_PART = 352
+SCALAR_CUT = 384
 
 
 def tile_mix_dwsav_sgd_kernel(tc, x4_words, x4_scales, x8, dy, w, out):
@@ -200,13 +201,15 @@ def tile_mix_dwsav_sgd_kernel(tc, x4_words, x4_scales, x8, dy, w, out):
         multiply(2, 2, True, False)
         multiply(0, 2, False, False)
         interleave_vector(1, 2, LAST_SHARE[2])
-        interleave_scalar(1, 2, LAST_SHARE[2], HALF)
-        interleave_scalar(1, 2, HALF, N)
+        prescale(0, 1)
+        interleave_scalar(1, 2, LAST_SHARE[2], SCALAR_CUT)
         prescale(1, 0)
+        prescale(1, 1)
+        interleave_scalar(1, 2, SCALAR_CUT, N)
         finish(0, 0)
+        finish(0, 1)
         quantize(1, 2, 0, HALF)
         multiply_bank(1, 2, 0, HALF, False, True)
-        finish(0, 1)
         finish(1, 0)
         quantize(1, 2, HALF, N)
         multiply_bank(1, 2, HALF, N, False, True)

@@ -24,7 +24,8 @@ STEP = -0.0625
 WHOLE_SHARE = (320, 288, 256)
 LAST_SHARE = (304, 304, 208)
 HALF = N // 2
-VECTOR_PART = 352
+QUARTER = N // 4
+ADD_SHARE = 128
 SCALAR_CUT = 384
 
 
@@ -128,17 +129,16 @@ def tile_mix_dwsav_sgd_kernel(tc, x4_words, x4_scales, x8, dy, w, out):
         scaled = {}
 
         def prescale(c, m):
-            scaled[c, m] = sbuf("y_%d_%d" % (c, m), [P, N - VECTOR_PART], F32)
-            nc.scalar.activation(out=scaled[c, m][:], in_=acc[c, 0, m][:, VECTOR_PART:N], func=COPY, scale=STEP)
+            scaled[c, m] = sbuf("y_%d_%d" % (c, m), [P, ADD_SHARE], F32)
+            hi = banks[c][0][1]
+            nc.scalar.activation(out=scaled[c, m][:], in_=acc[c, 0, m][:, hi - ADD_SHARE :], func=COPY, scale=STEP)
 
         def finish(c, m):
             o = sbuf("o_%d_%d" % (c, m), [P, N], F32)
-            part = N
-            if (c, m) in scaled:
-                part = VECTOR_PART
-                nc.gpsimd.tensor_tensor(out=o[:, part:N], in0=scaled[c, m][:], in1=w_sb[c, m][:, part:N], op=ADD)
-            for lo, hi in banks[c]:
-                hi = min(hi, part)
+            end = banks[c][0][1]
+            part = end - ADD_SHARE
+            nc.gpsimd.tensor_tensor(out=o[:, part:end], in0=scaled[c, m][:], in1=w_sb[c, m][:, part:end], op=ADD)
+            for lo, hi in ((0, part),) + banks[c][1:]:
                 nc.vector.scalar_tensor_tensor(
                     out=o[:, lo:hi],
                     in0=acc[c, lo, m][:, 0 : hi - lo],
@@ -201,15 +201,19 @@ def tile_mix_dwsav_sgd_kernel(tc, x4_words, x4_scales, x8, dy, w, out):
         multiply(2, 2, True, False)
         multiply(0, 2, False, False)
         interleave_vector(1, 2, LAST_SHARE[2])
+        prescale(0, 0)
         prescale(0, 1)
         interleave_scalar(1, 2, LAST_SHARE[2], SCALAR_CUT)
         prescale(1, 0)
         prescale(1, 1)
         interleave_scalar(1, 2, SCALAR_CUT, N)
         finish(0, 0)
+        quantize(1, 2, 0, QUARTER)
         finish(0, 1)
-        quantize(1, 2, 0, HALF)
+        quantize(1, 2, QUARTER, HALF)
         multiply_bank(1, 2, 0, HALF, False, True)
+        prescale(2, 0)
+        prescale(2, 1)
         finish(1, 0)
         quantize(1, 2, HALF, N)
         multiply_bank(1, 2, HALF, N, False, True)

@@ -20,11 +20,12 @@ P = 128
 N = 512
 D, H = 256, 1536
 ALIGN = 256
+DMA_ALIGN = 1024
 STEP = -0.0625
-WHOLE_SHARE = (320, 288, 256)
-LAST_SHARE = (304, 304, 208)
 HALF = N // 2
 QUARTER = N // 4
+WHOLE_SHARE = (320, 288, 256)
+LAST_SHARE = (304, 304, 208)
 ADD_SHARE = 128
 SCALAR_CUT = 384
 
@@ -36,10 +37,10 @@ def tile_mix_dwsav_sgd_kernel(tc, x4_words, x4_scales, x8, dy, w, out):
         psum = ctx.enter_context(tc.psum_pool(name="psum", bufs=1))
         ctx.enter_context(tc.manual_schedule())
 
-        def sbuf(name, shape, dtype):
-            return pool.tile(shape, dtype, name=name, align_bytes=ALIGN)
+        def sbuf(name, shape, dtype, align=ALIGN):
+            return pool.tile(shape, dtype, name=name, align_bytes=align)
 
-        acc, raw, grouped, codes, scales, w_sb, x4_wd = {}, {}, {}, {}, {}, {}, {}
+        acc, raw, grouped, codes, scales, w_sb, x4_wd, scaled = {}, {}, {}, {}, {}, {}, {}, {}
         banks = {0: ((0, N),), 1: ((0, N),), 2: ((0, HALF), (HALF, N))}
         for c in range(3):
             for lo, hi in banks[c]:
@@ -54,22 +55,19 @@ def tile_mix_dwsav_sgd_kernel(tc, x4_words, x4_scales, x8, dy, w, out):
         def rows_of(g):
             return dy[512 * g : 512 * (g + 1), :].rearrange("(p j) h -> p j h", j=4)
 
-        def pairs(t, pitch, c):
-            view = t[:, 0 : 2 * pitch * H].rearrange("p (a r h) -> p a r h", a=2, r=pitch)
-            return view[:, :, 0:2, N * c : N * (c + 1)]
+        def load_whole(g):
+            t = sbuf("raw_%d" % g, [P, 4 * H], F32, DMA_ALIGN)
+            nc.sync.dma_start(out=t[:], in_=rows_of(g).rearrange("p j h -> p (j h)"))
+            view = t[:].rearrange("p (a b h) -> p a b h", a=2, b=2)
+            for c in range(3):
+                raw[g, c] = view[:, :, :, N * c : N * (c + 1)]
 
         def load_x4_words(g):
-            x4_wd[g] = sbuf("x4_wd_%d" % g, [P, 2 * D], U8)
+            x4_wd[g] = sbuf("x4_wd_%d" % g, [P, 2 * D], U8, DMA_ALIGN)
             nc.sync.dma_start(out=x4_wd[g][:].bitcast(I32), in_=x4_words[g].bitcast(I32))
 
-        def load_whole(g):
-            t = sbuf("raw_%d" % g, [P, 4 * H], F32)
-            nc.sync.dma_start(out=t[:], in_=rows_of(g).rearrange("p j h -> p (j h)"))
-            for c in range(3):
-                raw[g, c] = pairs(t, 2, c)
-
         def load_staircase(g):
-            t = sbuf("raw_%d" % g, [P, 24 * N], F32)
+            t = sbuf("raw_%d" % g, [P, 24 * N], F32, DMA_ALIGN)
             first = t[:, 0 : 8 * N].rearrange("p (a x) -> p a x", a=2)
             raw[g, 0] = first.rearrange("p a (k n) -> p a k n", n=N)[:, :, 0:4:3, :]
             for c in (1, 2):
@@ -82,31 +80,27 @@ def tile_mix_dwsav_sgd_kernel(tc, x4_words, x4_scales, x8, dy, w, out):
                 nc.sync.dma_start(out=raw[g, c][:, :, 1, :], in_=by_pair[:, :, H + N * c : H + N * (c + 1)])
 
         def load_w(c, m):
-            w_sb[c, m] = sbuf("w_%d_%d" % (c, m), [P, N], F32)
+            w_sb[c, m] = sbuf("w_%d_%d" % (c, m), [P, N], F32, DMA_ALIGN)
             nc.sync.dma_start(out=w_sb[c, m][:], in_=w[P * m : P * (m + 1), N * c : N * (c + 1)])
 
-        def interleave_vector(g, c, hi, lo=0):
+        def interleave_vector(g, c, lo, hi):
             nc.vector.tensor_copy(
                 out=grouped[g, c][:, lo:hi, :].rearrange("p (n i) (a b) -> p n a b i", i=2, a=2),
                 in_=raw[g, c][:, :, :, lo:hi].rearrange("p a b (n i) -> p n a b i", i=2),
             )
 
-        def interleave_scalar(g, c, lo, hi=N):
+        def interleave_scalar(g, c, lo, hi):
             nc.scalar.copy(
                 out=grouped[g, c][:, lo:hi, :].rearrange("p (n i) (a b) -> p n a i b", i=8, a=2),
                 in_=raw[g, c][:, :, :, lo:hi].rearrange("p a b (n i) -> p n a i b", i=8),
             )
 
-        def quantize(g, c, lo=0, hi=N):
+        def quantize(g, c, lo, hi):
             nc.vector.quantize_mx(
                 out=codes[g, c][:, lo:hi].bitcast(E5M2),
                 scales=scales[g, c][:, lo:hi],
                 in_=grouped[g, c][:, lo:hi, :].rearrange("p h j -> p (h j)"),
             )
-
-        def multiply(g, c, start, stop):
-            for lo, hi in banks[c]:
-                multiply_bank(g, c, lo, hi, start, stop)
 
         def multiply_bank(g, c, lo, hi, start, stop):
             for m in range(2):
@@ -126,7 +120,9 @@ def tile_mix_dwsav_sgd_kernel(tc, x4_words, x4_scales, x8, dy, w, out):
                     stop=stop,
                 )
 
-        scaled = {}
+        def multiply(g, c, start, stop):
+            for lo, hi in banks[c]:
+                multiply_bank(g, c, lo, hi, start, stop)
 
         def prescale(c, m):
             scaled[c, m] = sbuf("y_%d_%d" % (c, m), [P, ADD_SHARE], F32)
@@ -134,7 +130,7 @@ def tile_mix_dwsav_sgd_kernel(tc, x4_words, x4_scales, x8, dy, w, out):
             nc.scalar.activation(out=scaled[c, m][:], in_=acc[c, 0, m][:, hi - ADD_SHARE :], func=COPY, scale=STEP)
 
         def finish(c, m):
-            o = sbuf("o_%d_%d" % (c, m), [P, N], F32)
+            o = sbuf("o_%d_%d" % (c, m), [P, N], F32, DMA_ALIGN)
             end = banks[c][0][1]
             part = end - ADD_SHARE
             nc.gpsimd.tensor_tensor(out=o[:, part:end], in0=scaled[c, m][:], in1=w_sb[c, m][:, part:end], op=ADD)
@@ -149,7 +145,7 @@ def tile_mix_dwsav_sgd_kernel(tc, x4_words, x4_scales, x8, dy, w, out):
                 )
             nc.sync.dma_start(out=out[P * m : P * (m + 1), N * c : N * (c + 1)], in_=o[:])
 
-        x4_sc = sbuf("x4_sc", [P, 2, D], U8)
+        x4_sc = sbuf("x4_sc", [P, 2, D], U8, DMA_ALIGN)
         nc.vector.memset(x4_sc[:].rearrange("p a n -> p (a n)").bitcast(I32), 0)
 
         load_whole(2)
@@ -159,7 +155,7 @@ def tile_mix_dwsav_sgd_kernel(tc, x4_words, x4_scales, x8, dy, w, out):
                 in_=x4_scales[:, 4 * q : 4 * q + 4, :].rearrange("a r n -> r a n").bitcast(I32),
             )
         load_whole(0)
-        x8_raw = sbuf("x8_raw", [P, 4, D], F32)
+        x8_raw = sbuf("x8_raw", [P, 4, D], F32, DMA_ALIGN)
         nc.sync.dma_start(out=x8_raw[:], in_=x8.rearrange("(p j) d -> p j d", j=4))
         load_staircase(1)
         for c in range(3):
@@ -171,36 +167,37 @@ def tile_mix_dwsav_sgd_kernel(tc, x4_words, x4_scales, x8, dy, w, out):
         x8_scales = sbuf("x8_scales", [P, D], U8)
 
         for g in (2, 0):
-            interleave_scalar(g, 0, WHOLE_SHARE[0])
-            interleave_scalar(g, 1, WHOLE_SHARE[1])
+            interleave_scalar(g, 0, WHOLE_SHARE[0], N)
+            interleave_scalar(g, 1, WHOLE_SHARE[1], N)
             if g == 0:
                 nc.scalar.copy(out=x8_grp[:], in_=x8_raw[:].rearrange("p j d -> p d j"))
-            interleave_scalar(g, 2, WHOLE_SHARE[2])
-            interleave_vector(g, 0, WHOLE_SHARE[0])
-            interleave_vector(g, 1, WHOLE_SHARE[1])
-            quantize(g, 0)
-            interleave_vector(g, 2, WHOLE_SHARE[2])
-            quantize(g, 1)
+            interleave_scalar(g, 2, WHOLE_SHARE[2], N)
+            interleave_vector(g, 0, 0, WHOLE_SHARE[0])
+            interleave_vector(g, 1, 0, WHOLE_SHARE[1])
+            quantize(g, 0, 0, N)
+            interleave_vector(g, 2, 0, WHOLE_SHARE[2])
+            quantize(g, 1, 0, N)
             if g == 0:
                 nc.vector.quantize_mx(
                     out=x8_codes[:].bitcast(E4M3), scales=x8_scales[:], in_=x8_grp[:].rearrange("p d j -> p (d j)")
                 )
-            quantize(g, 2)
+            quantize(g, 2, 0, N)
         for c in range(2):
             multiply(2, c, True, False)
 
         for c in range(2):
-            interleave_scalar(1, c, LAST_SHARE[c])
+            interleave_scalar(1, c, LAST_SHARE[c], N)
         for c in range(2):
-            interleave_vector(1, c, HALF)
-            interleave_vector(1, c, LAST_SHARE[c], HALF)
+            interleave_vector(1, c, 0, HALF)
+            interleave_vector(1, c, HALF, LAST_SHARE[c])
             quantize(1, c, 0, HALF)
             quantize(1, c, HALF, N)
             multiply(0, c, False, False)
             multiply(1, c, False, True)
         multiply(2, 2, True, False)
         multiply(0, 2, False, False)
-        interleave_vector(1, 2, LAST_SHARE[2])
+
+        interleave_vector(1, 2, 0, LAST_SHARE[2])
         prescale(0, 0)
         prescale(0, 1)
         interleave_scalar(1, 2, LAST_SHARE[2], SCALAR_CUT)

from contextlib import ExitStack

import concourse.mybir as mybir

FLOPS = 2 * 1536 * 256 * 1536

F32 = mybir.dt.float32
BF16 = mybir.dt.bfloat16
I32 = mybir.dt.int32
U32 = mybir.dt.uint32
U8 = mybir.dt.uint8
E4M3 = mybir.dt.float8_e4m3fn_x4
E5M2 = mybir.dt.float8_e5m2_x4
E2M1 = mybir.dt.float4_e2m1fn_x4
MULT = mybir.AluOpType.mult
ADD = mybir.AluOpType.add
COPY = mybir.ActivationFunctionType.Copy

P = 128
N = 512
D, H = 256, 1536
ALIGN = 256
DMA_ALIGN = 1024
STEP = -0.0625
HALF = N // 2
QUARTER = N // 4
WHOLE_SHARE = (320, 288, 256)
LAST_SHARE = (304, 304, 208)
ADD_SHARE = 128
SCALAR_CUT = 384


def tile_mix_dwsav_sgd_kernel(tc, x4_words, x4_scales, x8, dy, w, out):
    nc = tc.nc
    with ExitStack() as ctx:
        pool = ctx.enter_context(tc.tile_pool(name="pool", bufs=1))
        psum = ctx.enter_context(tc.psum_pool(name="psum", bufs=1))
        ctx.enter_context(tc.manual_schedule())

        def sbuf(name, shape, dtype, align=ALIGN):
            return pool.tile(shape, dtype, name=name, align_bytes=align)

        acc, raw, grouped, codes, scales, w_sb, x4_wd, scaled = {}, {}, {}, {}, {}, {}, {}, {}
        banks = {0: ((0, N),), 1: ((0, N),), 2: ((0, HALF), (HALF, N))}
        for c in range(3):
            for lo, hi in banks[c]:
                for m in range(2):
                    bank = psum.tile([P, N], F32, name="acc_%d_%d_%d" % (c, lo, m))
                    acc[c, lo, m] = bank[:, 0 : hi - lo]
            for g in range(3):
                grouped[g, c] = sbuf("grp_%d_%d" % (g, c), [P, N, 4], BF16)
                codes[g, c] = sbuf("cod_%d_%d" % (g, c), [P, N], U32)
                scales[g, c] = sbuf("sca_%d_%d" % (g, c), [P, N], U8)

        def rows_of(g):
            return dy[512 * g : 512 * (g + 1), :].rearrange("(p j) h -> p j h", j=4)

        def load_whole(g):
            t = sbuf("raw_%d" % g, [P, 4 * H], F32, DMA_ALIGN)
            nc.sync.dma_start(out=t[:], in_=rows_of(g).rearrange("p j h -> p (j h)"))
            view = t[:].rearrange("p (a b h) -> p a b h", a=2, b=2)
            for c in range(3):
                raw[g, c] = view[:, :, :, N * c : N * (c + 1)]

        def load_x4_words(g):
            x4_wd[g] = sbuf("x4_wd_%d" % g, [P, 2 * D], U8, DMA_ALIGN)
            nc.sync.dma_start(out=x4_wd[g][:].bitcast(I32), in_=x4_words[g].bitcast(I32))

        def load_staircase(g):
            t = sbuf("raw_%d" % g, [P, 24 * N], F32, DMA_ALIGN)
            first = t[:, 0 : 8 * N].rearrange("p (a x) -> p a x", a=2)
            raw[g, 0] = first.rearrange("p a (k n) -> p a k n", n=N)[:, :, 0:4:3, :]
            for c in (1, 2):
                view = t[:, 0 : 8 * (c + 1) * N].rearrange("p (b r k n) -> p r b k n", b=2, k=4, n=N)
                raw[g, c] = view[:, 0:2, :, c, :]
            by_pair = rows_of(g).rearrange("p (a b) h -> p a (b h)", a=2)
            nc.sync.dma_start(out=first, in_=by_pair[:, :, 0 : H + N])
            for c in (1, 2):
                load_x4_words(c - 1)
                nc.sync.dma_start(out=raw[g, c][:, :, 1, :], in_=by_pair[:, :, H + N * c : H + N * (c + 1)])

        def load_w(c, m):
            w_sb[c, m] = sbuf("w_%d_%d" % (c, m), [P, N], F32, DMA_ALIGN)
            nc.sync.dma_start(out=w_sb[c, m][:], in_=w[P * m : P * (m + 1), N * c : N * (c + 1)])

        def interleave_vector(g, c, lo, hi):
            nc.vector.tensor_copy(
                out=grouped[g, c][:, lo:hi, :].rearrange("p (n i) (a b) -> p n a b i", i=2, a=2),
                in_=raw[g, c][:, :, :, lo:hi].rearrange("p a b (n i) -> p n a b i", i=2),
            )

        def interleave_scalar(g, c, lo, hi):
            nc.scalar.copy(
                out=grouped[g, c][:, lo:hi, :].rearrange("p (n i) (a b) -> p n a i b", i=8, a=2),
                in_=raw[g, c][:, :, :, lo:hi].rearrange("p a b (n i) -> p n a i b", i=8),
            )

        def quantize(g, c, lo, hi):
            nc.vector.quantize_mx(
                out=codes[g, c][:, lo:hi].bitcast(E5M2),
                scales=scales[g, c][:, lo:hi],
                in_=grouped[g, c][:, lo:hi, :].rearrange("p h j -> p (h j)"),
            )

        def multiply_bank(g, c, lo, hi, start, stop):
            for m in range(2):
                if g == 2:
                    lhsT = x8_codes[:, P * m : P * (m + 1)].bitcast(E4M3)
                    lhsT_scale = x8_scales[:, P * m : P * (m + 1)]
                else:
                    lhsT = x4_wd[g][:, 2 * P * m : 2 * P * (m + 1)].bitcast(E2M1)
                    lhsT_scale = x4_sc[:, g, P * m : P * (m + 1)]
                nc.tensor.matmul_mx(
                    out=acc[c, lo, m],
                    lhsT=lhsT,
                    lhsT_scale=lhsT_scale,
                    rhs=codes[g, c][:, lo:hi].bitcast(E5M2),
                    rhs_scale=scales[g, c][:, lo:hi],
                    start=start,
                    stop=stop,
                )

        def multiply(g, c, start, stop):
            for lo, hi in banks[c]:
                multiply_bank(g, c, lo, hi, start, stop)

        def prescale(c, m):
            scaled[c, m] = sbuf("y_%d_%d" % (c, m), [P, ADD_SHARE], F32)
            hi = banks[c][0][1]
            nc.scalar.activation(out=scaled[c, m][:], in_=acc[c, 0, m][:, hi - ADD_SHARE :], func=COPY, scale=STEP)

        def finish(c, m):
            o = sbuf("o_%d_%d" % (c, m), [P, N], F32, DMA_ALIGN)
            end = banks[c][0][1]
            part = end - ADD_SHARE
            nc.gpsimd.tensor_tensor(out=o[:, part:end], in0=scaled[c, m][:], in1=w_sb[c, m][:, part:end], op=ADD)
            for lo, hi in ((0, part),) + banks[c][1:]:
                nc.vector.scalar_tensor_tensor(
                    out=o[:, lo:hi],
                    in0=acc[c, lo, m][:, 0 : hi - lo],
                    scalar=STEP,
                    in1=w_sb[c, m][:, lo:hi],
                    op0=MULT,
                    op1=ADD,
                )
            nc.sync.dma_start(out=out[P * m : P * (m + 1), N * c : N * (c + 1)], in_=o[:])

        x4_sc = sbuf("x4_sc", [P, 2, D], U8, DMA_ALIGN)
        nc.vector.memset(x4_sc[:].rearrange("p a n -> p (a n)").bitcast(I32), 0)

        load_whole(2)
        for q in range(4):
            nc.sync.dma_start(
                out=x4_sc[32 * q : 32 * q + 4, :, :].bitcast(I32),
                in_=x4_scales[:, 4 * q : 4 * q + 4, :].rearrange("a r n -> r a n").bitcast(I32),
            )
        load_whole(0)
        x8_raw = sbuf("x8_raw", [P, 4, D], F32, DMA_ALIGN)
        nc.sync.dma_start(out=x8_raw[:], in_=x8.rearrange("(p j) d -> p j d", j=4))
        load_staircase(1)
        for c in range(3):
            for m in range(2):
                load_w(c, m)

        x8_grp = sbuf("x8_grp", [P, D, 4], BF16)
        x8_codes = sbuf("x8_codes", [P, D], U32)
        x8_scales = sbuf("x8_scales", [P, D], U8)

        for g in (2, 0):
            interleave_scalar(g, 0, WHOLE_SHARE[0], N)
            interleave_scalar(g, 1, WHOLE_SHARE[1], N)
            if g == 0:
                nc.scalar.copy(out=x8_grp[:], in_=x8_raw[:].rearrange("p j d -> p d j"))
            interleave_scalar(g, 2, WHOLE_SHARE[2], N)
            interleave_vector(g, 0, 0, WHOLE_SHARE[0])
            interleave_vector(g, 1, 0, WHOLE_SHARE[1])
            quantize(g, 0, 0, N)
            interleave_vector(g, 2, 0, WHOLE_SHARE[2])
            quantize(g, 1, 0, N)
            if g == 0:
                nc.vector.quantize_mx(
                    out=x8_codes[:].bitcast(E4M3), scales=x8_scales[:], in_=x8_grp[:].rearrange("p d j -> p (d j)")
                )
            quantize(g, 2, 0, N)
        for c in range(2):
            multiply(2, c, True, False)

        for c in range(2):
            interleave_scalar(1, c, LAST_SHARE[c], N)
        for c in range(2):
            interleave_vector(1, c, 0, HALF)
            interleave_vector(1, c, HALF, LAST_SHARE[c])
            quantize(1, c, 0, HALF)
            quantize(1, c, HALF, N)
            multiply(0, c, False, False)
            multiply(1, c, False, True)
        multiply(2, 2, True, False)
        multiply(0, 2, False, False)

        interleave_vector(1, 2, 0, LAST_SHARE[2])
        prescale(0, 0)
        prescale(0, 1)
        interleave_scalar(1, 2, LAST_SHARE[2], SCALAR_CUT)
        prescale(1, 0)
        prescale(1, 1)
        interleave_scalar(1, 2, SCALAR_CUT, N)
        finish(0, 0)
        quantize(1, 2, 0, QUARTER)
        finish(0, 1)
        quantize(1, 2, QUARTER, HALF)
        multiply_bank(1, 2, 0, HALF, False, True)
        prescale(2, 0)
        prescale(2, 1)
        finish(1, 0)
        quantize(1, 2, HALF, N)
        multiply_bank(1, 2, HALF, N, False, True)
        finish(1, 1)
        finish(2, 0)
        finish(2, 1)
